import numpy as np
import ml_dtypes


def mxq(x, axis, fmt="e4m3"):
    dtype, down = {"e4m3": (ml_dtypes.float8_e4m3fn, 7), "e5m2": (ml_dtypes.float8_e5m2, 14)}[fmt]
    v = np.moveaxis(np.asarray(x, np.float32).astype(ml_dtypes.bfloat16).astype(np.float64), axis, -1)
    blocks = v.reshape(v.shape[:-1] + (-1, 32))
    amax = np.abs(blocks).max(-1, keepdims=True)
    byte = np.maximum(np.where(amax > 0, np.frexp(amax)[1] - 1 + 127, 0) - down, 1)
    scale = np.exp2(byte - 127.0)
    codes = (blocks / scale).astype(np.float32).astype(dtype).astype(np.float64)
    return np.moveaxis((codes * scale).reshape(v.shape), -1, axis)


WIDE = False


def mx_kscale(k):
    if not WIDE:
        return np.ones(k)
    levels = np.array([10, -10, 5, -5, 0])
    if k % 512:
        return np.exp2(np.random.permutation(np.resize(levels, k // 32))).repeat(32)
    a = np.empty((k // 512, 16))
    for p in range(k // 512):
        a[p, :8] = np.random.permutation(np.resize(levels, 8))
        for g in range(8):
            far = levels[np.abs(levels - a[p, g]) >= 10]
            a[p, g + 8] = far[np.random.randint(len(far))]
    return np.exp2(a.ravel()).repeat(32)


def f64(x):
    return np.asarray(x).astype(np.float64)


def striped(idx):
    return np.tile(idx.reshape(-1, 16).T, (8, 1)).astype(np.uint16)


def unstriped(offs):
    return offs[:16].T.reshape(-1).astype(np.int64)


E2M1 = np.array([0.0, 0.5, 1.0, 1.5, 2.0, 3.0, 4.0, 6.0, -0.0, -0.5, -1.0, -1.5, -2.0, -3.0, -4.0, -6.0])


def pack_weight(w, fmt):
    k, n = w.shape
    w = f64(np.asarray(w, np.float32).astype(ml_dtypes.bfloat16)).reshape(k // 32, 32, n)
    amax = np.abs(w).max(1)
    if fmt == "e4m3":
        byte = np.frexp(amax)[1] - 1 + 127 - 7
    else:
        mant, ex = np.frexp(amax / 6.0)
        byte = np.where(mant > 0.5, ex, ex - 1) + 127
    byte = np.clip(np.where(amax > 0, byte, 1), 1, 254)
    scaled = (w * np.exp2(127.0 - byte)[:, None, :]).reshape(k, n).astype(np.float32)
    by_word = np.ascontiguousarray(scaled.reshape(k // 512, 128, 4, n).transpose(0, 1, 3, 2))
    if fmt == "e4m3":
        words = by_word.astype(ml_dtypes.float8_e4m3fn).view(np.uint8)
    else:
        c = by_word.astype(ml_dtypes.float4_e2m1fn).view(np.uint8) & 0xF
        words = (c[..., 0::2] | (c[..., 1::2] << 4)).reshape(k // 512, 128, 2 * n)
    return np.ascontiguousarray(words), np.ascontiguousarray(byte.astype(np.uint8).reshape(k // 512, 16, n))


def unpack_weight(words, scales, fmt):
    g, _, n = scales.shape
    words = np.ascontiguousarray(words).reshape(g, 128, n, -1)
    if fmt == "e4m3":
        vals = words.view(ml_dtypes.float8_e4m3fn).astype(np.float64)
    else:
        nib = np.empty((g, 128, n, 4), np.uint8)
        nib[..., 0::2] = words & 0xF
        nib[..., 1::2] = words >> 4
        vals = E2M1[nib]
    vals = vals * np.repeat(np.exp2(scales.astype(np.float64) - 127.0), 8, axis=1)[..., None]
    return vals.transpose(0, 1, 3, 2).reshape(g * 512, n)


def gelu(v):
    return 0.5 * v * (1.0 + np.tanh(np.sqrt(2.0 / np.pi) * (v + 0.044715 * v**3)))


def bf(x):
    return np.asarray(x, np.float32).astype(ml_dtypes.bfloat16)


def planes(Y):
    n, m = Y.shape
    b = f64(bf(Y)).reshape(n // 32, 32, m)
    amax = np.abs(b).max(1)
    byte = np.clip(np.where(amax > 0, np.frexp(amax)[1] - 1 + 127 - 7, 1), 1, 254)
    codes = (b * np.exp2(127.0 - byte)[:, None, :]).reshape(n, m).astype(np.float32).astype(ml_dtypes.float8_e4m3fn).view(np.uint8)
    words = codes.reshape(n // 512, 128, 4, m).transpose(0, 1, 3, 2)
    return np.ascontiguousarray(words), np.ascontiguousarray(byte.astype(np.uint8).reshape(n // 512, 16, m))


K, T, S, P, H = 1536, 4096, 1024, 512, 1024


def setup_inputs():
    n = np.random.standard_normal
    s = mx_kscale(K)[:, None]
    u = mx_kscale(H)[:, None]
    d = {}
    d["tab_words"], d["tab_scales"] = pack_weight(n((K, T)) * s, "e4m3")
    d["offs"] = striped(np.random.permutation(T)[:S])
    perm = np.random.permutation(S)
    d["pos1"] = striped(perm[:P])
    d["pos2"] = striped(perm[P:2 * P])
    d["w1"] = (n((K, H)) / K**0.5 / s).astype(np.float32)
    d["floor_v"] = (0.5 * n(H) - 0.3).astype(np.float32)
    d["gain"] = (np.exp(0.3 * n(H)) * u[:, 0]).astype(np.float32)
    d["w2_words"], d["w2_scales"] = pack_weight(2.2 * n((H, H)) / H**0.5 / u, "e2m1")
    d["site"] = (1.2 * n((H, S)) / u).astype(np.float32)
    d["span"] = np.exp(0.8 * n(H)).astype(np.float32)
    return d


def reference(tab_words, tab_scales, offs, pos1, pos2, w1, floor_v, gain, w2_words, w2_scales, site, span):
    v = unpack_weight(tab_words, tab_scales, "e4m3")[:, unstriped(offs)]
    flow = mxq(f64(w1), 0, "e4m3").T @ v
    h = np.maximum(flow, f64(floor_v)[:, None]) * f64(gain)[:, None]
    w2 = unpack_weight(w2_words, w2_scales, "e2m1")
    mixed = (w2.T @ mxq(h, 0, "e4m3")) + h * f64(site)
    g2 = 1.0 / (1.0 + np.exp(-mixed))
    y = f64(span)[:, None] * (g2[:, unstriped(pos1)] - g2[:, unstriped(pos2)])
    words, scales = planes(y)
    return y, words, scales

@@ -1,0 +1,313 @@
+from contextlib import ExitStack
+
+import concourse.mybir as mybir
+
+K, T, S, PAIRS, H = 1536, 4096, 1024, 512, 1024
+FLOPS = 2 * K * H * S + 2 * H * H * S
+
+F32 = mybir.dt.float32
+BF16 = mybir.dt.bfloat16
+I32 = mybir.dt.int32
+U32 = mybir.dt.uint32
+U16 = mybir.dt.uint16
+U8 = mybir.dt.uint8
+FP8X4 = mybir.dt.float8_e4m3fn_x4
+FP4X4 = mybir.dt.float4_e2m1fn_x4
+ALU = mybir.AluOpType
+ACT = mybir.ActivationFunctionType
+
+P = 128
+PACK = 4
+PASS = P * PACK
+NB = 512
+KP = K // PASS
+HG = H // PASS
+JH = S // NB
+
+
+def tile_list_tapping_panel_contrast_kernel(
+    tc, tab_words, tab_scales, offs, pos1, pos2, w1, floor_v, gain, w2_words, w2_scales, site, span,
+    out_0, out_1, out_2,
+):
+    nc = tc.nc
+    with ExitStack() as ctx:
+        keep = ctx.enter_context(tc.tile_pool(name="keep", bufs=1))
+        psum = ctx.enter_context(tc.psum_pool(name="psum", bufs=8))
+        with tc.tile_pool(name="early", bufs=1) as early:
+
+            def kt(name, shape, dtype):
+                return keep.tile(shape, dtype, name=name, align_bytes=64)
+
+            def et(name, shape, dtype):
+                return early.tile(shape, dtype, name=name, align_bytes=64)
+
+            offs_sb = keep.tile([P, S // 16], U16, name="offs_sb")
+            pos1_sb = keep.tile([P, PAIRS // 16], U16, name="pos1_sb")
+            pos2_sb = keep.tile([P, PAIRS // 16], U16, name="pos2_sb")
+            floor_sb = kt("floor_sb", [P, HG, PACK], F32)
+            gain_sb = kt("gain_sb", [P, HG, PACK], F32)
+            span_sb = kt("span_sb", [P, HG, PACK], F32)
+            warm = kt("warm", [P, 2], F32)
+
+            tabw = [et("tabw%d" % a, [P, T], U32) for a in range(KP)]
+            tabs = et("tabs", [P, T], U8)
+            w2w_raw = et("w2w_raw", [P, HG, 2 * H], U8)
+            w2s_raw = et("w2s_raw", [P, HG, H], U8)
+            w1_raw = {(b, a): et("w1raw%d%d" % (b, a), [P, PACK, PASS], F32) for b in range(HG) for a in range(KP)}
+
+            vw = [kt("vw%d" % a, [P, S], U32) for a in range(KP)]
+            vs = kt("vs", [P, S], U8)
+            w2w = kt("w2w", [P, HG, 2 * H], U8)
+            w2s = kt("w2s", [P, HG, H], U8)
+            w1q = {(b, a): kt("w1q%d%d" % (b, a), [P, PASS], U32) for b in range(HG) for a in range(KP)}
+            w1s = {(b, a): kt("w1s%d%d" % (b, a), [P, PASS], U8) for b in range(HG) for a in range(KP)}
+            site_sb = {(b, t): kt("site%d%d" % (b, t), [P, S], F32) for b in range(HG) for t in range(PACK)}
+            h_sb = {(b, j): kt("h%d%d" % (b, j), [P, PACK, NB], F32) for b in range(HG) for j in range(JH)}
+            hq = {(b, j): kt("hq%d%d" % (b, j), [P, NB], U32) for b in range(HG) for j in range(JH)}
+            hs = {(b, j): kt("hs%d%d" % (b, j), [P, NB], U8) for b in range(HG) for j in range(JH)}
+
+            nc.vector.memset(tabs[:].bitcast(I32), 0)
+            nc.vector.memset(w2s_raw[:].rearrange("p a c -> p (a c)").bitcast(I32), 0)
+            nc.vector.memset(warm[:, 0:1], 0.0)
+            nc.scalar.activation(out=warm[:, 1:2], in_=warm[:, 0:1], func=ACT.Sigmoid)
+
+            def load_tab(a):
+                nc.sync.dma_start(out=tabw[a][:].bitcast(I32), in_=tab_words[a].rearrange("p t i -> p (t i)").bitcast(I32))
+
+            def load_w1(b, a):
+                rows = w1[PASS * a : PASS * (a + 1), PASS * b : PASS * (b + 1)]
+                nc.sync.dma_start(out=w1_raw[b, a][:], in_=rows.rearrange("(p j) c -> p j c", j=PACK))
+
+            def load_vec(dst, vec):
+                nc.sync.dma_start(out=dst[:], in_=vec.rearrange("(b p t) -> p b t", p=P, t=PACK))
+
+            load_tab(0)
+            nc.sync.dma_start(offs_sb[:], offs)
+            nc.sync.dma_start(out=w2w_raw[:].bitcast(I32), in_=w2_words.rearrange("a p c -> p a c").bitcast(I32))
+            for q in range(4):
+                nc.sync.dma_start(
+                    out=tabs[32 * q : 32 * q + 4 * KP, :].bitcast(I32),
+                    in_=tab_scales[:, 4 * q : 4 * q + 4, :].bitcast(I32),
+                )
+            load_w1(0, 0)
+            for q in range(4):
+                nc.sync.dma_start(
+                    out=w2s_raw[32 * q : 32 * q + 4, :, :].bitcast(I32),
+                    in_=w2_scales[:, 4 * q : 4 * q + 4, :].rearrange("a r c -> r a c").bitcast(I32),
+                )
+            load_tab(1)
+            load_vec(floor_sb, floor_v)
+            load_vec(gain_sb, gain)
+            load_w1(0, 1)
+            load_tab(2)
+            load_w1(0, 2)
+            for a in range(KP):
+                load_w1(1, a)
+            site_rows = site.rearrange("(b p t) j -> b t p j", p=P, t=PACK)
+            for b in range(HG):
+                for t in range(PACK):
+                    nc.sync.dma_start(out=site_sb[b, t][:], in_=site_rows[b, t])
+                if b == 0:
+                    nc.sync.dma_start(pos1_sb[:], pos1)
+                    nc.sync.dma_start(pos2_sb[:], pos2)
+                    load_vec(span_sb, span)
+
+            w1_bf = {}
+
+            def cast_w1(b, a, vector_slots):
+                tile = early.tile([P, PASS * PACK], BF16, name="w1bf", tag="w1bf", bufs=2, align_bytes=64)
+                w1_bf[b, a] = tile
+                dst = tile[:].rearrange("p (t m j) -> p m j t", t=PACK, j=PACK)
+                src = w1_raw[b, a][:].rearrange("p j (m t) -> p m j t", t=PACK)
+                if vector_slots > 0:
+                    nc.vector.tensor_copy(out=dst[:, :, :, 0:vector_slots], in_=src[:, :, :, 0:vector_slots])
+                if vector_slots < PACK:
+                    nc.scalar.copy(out=dst[:, :, :, vector_slots:PACK], in_=src[:, :, :, vector_slots:PACK])
+
+            def quant_w1(b, a):
+                nc.vector.quantize_mx(out=w1q[b, a][:].bitcast(FP8X4), scales=w1s[b, a][:], in_=w1_bf[b, a][:])
+
+            def gather_words(a):
+                nc.vector.tensor_copy(vw[a][:], tabw[a][:].indirect(offs_sb[:]))
+
+            flow = {}
+
+            def stage1(b, a, j, t):
+                if a == 0:
+                    flow[b, j, t] = psum.tile([P, NB], F32, name="acc", tag="acc")
+                cols = slice(P * t, P * (t + 1))
+                toks = slice(NB * j, NB * (j + 1))
+                nc.tensor.matmul_mx(
+                    out=flow[b, j, t][:],
+                    lhsT=w1q[b, a][:, cols].bitcast(FP8X4), lhsT_scale=w1s[b, a][:, cols],
+                    rhs=vw[a][:, toks].bitcast(FP8X4), rhs_scale=vs[4 * a : P, toks],
+                    start=(a == 0), stop=(a == KP - 1),
+                )
+
+            def stage1_all(b, a):
+                for j in range(JH):
+                    for t in range(PACK):
+                        stage1(b, a, j, t)
+
+            def features(b, j, t):
+                nc.vector.tensor_scalar(
+                    out=h_sb[b, j][:, t, :], in0=flow[b, j, t][:],
+                    scalar1=floor_sb[:, b, t : t + 1], scalar2=gain_sb[:, b, t : t + 1],
+                    op0=ALU.max, op1=ALU.mult,
+                )
+
+            h_bf = {}
+
+            def weave(dst, src, lo, hi, engine):
+                d = dst.rearrange("p (c i t) -> p c t i", i=4, t=PACK)[:, lo // 4 : hi // 4]
+                s = src.rearrange("p t (c i) -> p c t i", i=4)[:, lo // 4 : hi // 4]
+                if engine == "v":
+                    nc.vector.tensor_copy(out=d, in_=s)
+                else:
+                    nc.scalar.copy(out=d, in_=s)
+
+            def weave_h(b, j, vector_cols):
+                tile = keep.tile([P, NB * PACK], BF16, name="hbf", tag="hbf", bufs=2, align_bytes=64)
+                h_bf[b, j] = tile
+                if vector_cols > 0:
+                    weave(tile[:], h_sb[b, j][:], 0, vector_cols, "v")
+                if vector_cols < NB:
+                    weave(tile[:], h_sb[b, j][:], vector_cols, NB, "s")
+
+            def quant_h(b, j):
+                nc.vector.quantize_mx(out=hq[b, j][:].bitcast(FP8X4), scales=hs[b, j][:], in_=h_bf[b, j][:])
+
+            def times_site(b, t):
+                for j in range(JH):
+                    part = site_sb[b, t][:, NB * j : NB * (j + 1)]
+                    nc.gpsimd.tensor_tensor(out=part, in0=h_sb[b, j][:, t, :], in1=part, op=ALU.mult)
+
+            gather_words(0)
+            cast_w1(0, 0, 0)
+            nc.vector.tensor_copy(vs[:], tabs[:].indirect(offs_sb[:]))
+            quant_w1(0, 0)
+            nc.vector.tensor_copy(
+                out=w2w[:].rearrange("p a (g t m e) -> p (a g) m t e", g=HG, t=PACK, e=2),
+                in_=w2w_raw[:].rearrange("p a (g m t e) -> p (a g) m t e", g=HG, t=PACK, e=2),
+            )
+            nc.vector.tensor_copy(
+                out=w2s[:].rearrange("p a (g t m) -> p (a g) m t", g=HG, t=PACK),
+                in_=w2s_raw[:].rearrange("p a (g m t) -> p (a g) m t", g=HG, t=PACK),
+            )
+            stage1_all(0, 0)
+            gather_words(1)
+            cast_w1(0, 1, 0)
+            quant_w1(0, 1)
+            stage1_all(0, 1)
+            gather_words(2)
+            cast_w1(0, 2, 3)
+            quant_w1(0, 2)
+            stage1_all(0, 2)
+
+            cast_w1(1, 0, 0)
+            for t in range(PACK):
+                features(0, 0, t)
+            quant_w1(1, 0)
+            cast_w1(1, 1, 0)
+            for t in range(PACK):
+                features(0, 1, t)
+            stage1_all(1, 0)
+            cast_w1(1, 2, 3)
+            quant_w1(1, 1)
+            stage1_all(1, 1)
+            quant_w1(1, 2)
+            stage1_all(1, 2)
+        late = ctx.enter_context(tc.tile_pool(name="late", bufs=1))
+
+        weave_h(0, 0, 0)
+        for t in range(PACK):
+            features(1, 0, t)
+        weave_h(0, 1, 0)
+        quant_h(0, 0)
+        for t in range(PACK):
+            features(1, 1, t)
+        weave_h(1, 0, 0)
+        quant_h(0, 1)
+        weave_h(1, 1, 512)
+        quant_h(1, 0)
+        quant_h(1, 1)
+
+        gate = {}
+
+        def stage2(g, t):
+            times_site(g, t)
+            mixed = [psum.tile([P, NB], F32, name="acc", tag="acc") for j in range(JH)]
+            c0 = PASS * g + P * t
+            for a in range(HG):
+                for j in range(JH):
+                    nc.tensor.matmul_mx(
+                        out=mixed[j][:],
+                        lhsT=w2w[:, a, 2 * c0 : 2 * (c0 + P)].bitcast(FP4X4), lhsT_scale=w2s[:, a, c0 : c0 + P],
+                        rhs=hq[a, j][:].bitcast(FP8X4), rhs_scale=hs[a, j][:],
+                        start=(a == 0), stop=(a == HG - 1),
+                    )
+            for j in range(JH):
+                part = site_sb[g, t][:, NB * j : NB * (j + 1)]
+                nc.vector.tensor_tensor(out=part, in0=mixed[j][:], in1=part, op=ALU.add)
+            gate[g, t] = late.tile([P, S], F32, name="gate", tag="gate", bufs=6)
+            nc.scalar.activation(out=gate[g, t][:], in_=site_sb[g, t][:], func=ACT.Sigmoid)
+
+        y_sb = {}
+        yq = [late.tile([P, PAIRS], U32, name="yq%d" % g, align_bytes=64) for g in range(HG)]
+        ys = [late.tile([P, PAIRS], U8, name="ys%d" % g, align_bytes=64) for g in range(HG)]
+        y_rows = out_0.rearrange("(g p t) m -> g p t m", p=P, t=PACK)
+
+        def contrast(g, t, lo, hi):
+            n = hi - lo
+            if t == 0:
+                y_sb[g, lo] = late.tile([P, PACK, n], F32, name="y%d_%d" % (g, lo), align_bytes=64)
+            rest = late.tile([P, n], F32, name="rest", tag="rest", bufs=2)
+            diff = late.tile([P, n], F32, name="diff", tag="diff", bufs=3)
+            nc.vector.tensor_copy(rest[:], gate[g, t][:].indirect(pos2_sb[:, lo // 16 : hi // 16]))
+            nc.vector.tensor_tensor(diff[:], gate[g, t][:].indirect(pos1_sb[:, lo // 16 : hi // 16]), rest[:], ALU.subtract)
+            nc.scalar.activation(out=y_sb[g, lo][:, t, :], in_=diff[:], func=ACT.Copy, scale=span_sb[:, g, t : t + 1])
+            nc.sync.dma_start(out=y_rows[g][:, t, lo:hi], in_=y_sb[g, lo][:, t, :])
+
+        y_bf = {}
+
+        def weave_y(g, lo, hi, engine):
+            n = hi - lo
+            y_bf[g, lo] = late.tile([P, n * PACK], BF16, name="ybf%d_%d" % (g, lo), align_bytes=64)
+            weave(y_bf[g, lo][:], y_sb[g, lo][:], 0, n, engine)
+
+        def planes(g, lo, hi):
+            nc.vector.quantize_mx(out=yq[g][:, lo:hi].bitcast(FP8X4), scales=ys[g][:, lo:hi], in_=y_bf[g, lo][:])
+            words = out_1[g].rearrange("p m t -> p (m t)").bitcast(I32)
+            nc.sync.dma_start(out=words[:, lo:hi], in_=yq[g][:, lo:hi].bitcast(I32))
+            if hi == PAIRS:
+                for q in range(4):
+                    queue = nc.sync if q % 2 == 0 else nc.scalar
+                    queue.dma_start(
+                        out=out_2[g, 4 * q : 4 * q + 4, :].bitcast(I32),
+                        in_=ys[g][32 * q : 32 * q + 4, :].bitcast(I32),
+                    )
+
+        half = PAIRS // 2
+        stage2(0, 0)
+        for t in range(PACK):
+            if t + 1 < PACK:
+                stage2(0, t + 1)
+            else:
+                stage2(1, 0)
+            contrast(0, t, 0, PAIRS)
+        weave_y(0, 0, PAIRS, "s")
+        for t in range(PACK):
+            if t + 1 < PACK:
+                stage2(1, t + 1)
+            else:
+                contrast(1, 0, half, PAIRS)
+            contrast(1, t, 0, half)
+            if t == 1:
+                planes(0, 0, PAIRS)
+        weave_y(1, 0, half, "s")
+        contrast(1, 1, half, PAIRS)
+        contrast(1, 2, half, PAIRS)
+        planes(1, 0, half)
+        contrast(1, 3, half, PAIRS)
+        weave_y(1, half, PAIRS, "v")
+        planes(1, half, PAIRS)

@@ -124,15 +124,20 @@ def tile_list_tapping_panel_contrast_kernel(
                 if vector_slots < PACK:
                     nc.scalar.copy(out=dst[:, :, :, vector_slots:PACK], in_=src[:, :, :, vector_slots:PACK])
 
-            def quant_w1(b, a):
-                nc.vector.quantize_mx(out=w1q[b, a][:].bitcast(FP8X4), scales=w1s[b, a][:], in_=w1_bf[b, a][:])
+            def quant_w1(b, a, parts=1):
+                n = PASS // parts
+                for lo in range(0, PASS, n):
+                    nc.vector.quantize_mx(
+                        out=w1q[b, a][:, lo : lo + n].bitcast(FP8X4), scales=w1s[b, a][:, lo : lo + n],
+                        in_=w1_bf[b, a][:, PACK * lo : PACK * (lo + n)],
+                    )
 
             def gather_words(a):
                 nc.vector.tensor_copy(vw[a][:], tabw[a][:].indirect(offs_sb[:]))
 
             flow = {}
 
-            def stage1(b, a, j, t):
+            def stage1(b, a, j, t, stop):
                 if a == 0:
                     flow[b, j, t] = psum.tile([P, NB], F32, name="acc", tag="acc")
                 cols = slice(P * t, P * (t + 1))
@@ -141,13 +146,13 @@ def tile_list_tapping_panel_contrast_kernel(
                     out=flow[b, j, t][:],
                     lhsT=w1q[b, a][:, cols].bitcast(FP8X4), lhsT_scale=w1s[b, a][:, cols],
                     rhs=vw[a][:, toks].bitcast(FP8X4), rhs_scale=vs[4 * a : P, toks],
-                    start=(a == 0), stop=(a == KP - 1),
+                    start=(a == 0), stop=stop,
                 )
 
             def stage1_all(b, a):
                 for j in range(JH):
                     for t in range(PACK):
-                        stage1(b, a, j, t)
+                        stage1(b, a, j, t, a == KP - 1)
 
             def features(b, j, t):
                 nc.vector.tensor_scalar(
@@ -167,20 +172,16 @@ def tile_list_tapping_panel_contrast_kernel(
                     nc.scalar.copy(out=d, in_=s)
 
             def weave_h(b, j, vector_cols):
-                tile = keep.tile([P, NB * PACK], BF16, name="hbf", tag="hbf", bufs=2, align_bytes=64)
+                pool = late if (b, j) == (1, 1) else keep
+                tile = pool.tile([P, NB * PACK], BF16, name="hbf", tag="work%d" % (JH * b + j), align_bytes=64)
                 h_bf[b, j] = tile
-                if vector_cols > 0:
-                    weave(tile[:], h_sb[b, j][:], 0, vector_cols, "v")
+                for lo in range(0, vector_cols, 256):
+                    weave(tile[:], h_sb[b, j][:], lo, min(lo + 256, vector_cols), "v")
                 if vector_cols < NB:
                     weave(tile[:], h_sb[b, j][:], vector_cols, NB, "s")
 
             def quant_h(b, j):
                 nc.vector.quantize_mx(out=hq[b, j][:].bitcast(FP8X4), scales=hs[b, j][:], in_=h_bf[b, j][:])
-
-            def times_site(b, t):
-                for j in range(JH):
-                    part = site_sb[b, t][:, NB * j : NB * (j + 1)]
-                    nc.gpsimd.tensor_tensor(out=part, in0=h_sb[b, j][:, t, :], in1=part, op=ALU.mult)
 
             gather_words(0)
             cast_w1(0, 0, 0)
@@ -201,7 +202,7 @@ def tile_list_tapping_panel_contrast_kernel(
             stage1_all(0, 1)
             gather_words(2)
             cast_w1(0, 2, 3)
-            quant_w1(0, 2)
+            quant_w1(0, 2, 2)
             stage1_all(0, 2)
 
             cast_w1(1, 0, 0)
@@ -211,31 +212,45 @@ def tile_list_tapping_panel_contrast_kernel(
             cast_w1(1, 1, 0)
             for t in range(PACK):
                 features(0, 1, t)
-            stage1_all(1, 0)
-            cast_w1(1, 2, 3)
+            for t in range(PACK):
+                stage1(1, 0, 0, t, False)
             quant_w1(1, 1)
-            stage1_all(1, 1)
-            quant_w1(1, 2)
-            stage1_all(1, 2)
+            cast_w1(1, 2, 3)
+            quant_w1(1, 2, 2)
+            for a in range(1, KP):
+                for t in range(PACK):
+                    stage1(1, a, 0, t, a == KP - 1)
+            for t in range(PACK):
+                for a in (0, 2, 1):
+                    stage1(1, a, 1, t, a == 1)
         late = ctx.enter_context(tc.tile_pool(name="late", bufs=1))
 
         weave_h(0, 0, 0)
         for t in range(PACK):
             features(1, 0, t)
         weave_h(0, 1, 0)
-        quant_h(0, 0)
         for t in range(PACK):
             features(1, 1, t)
         weave_h(1, 0, 0)
+        quant_h(0, 0)
         quant_h(0, 1)
         weave_h(1, 1, 512)
         quant_h(1, 0)
         quant_h(1, 1)
 
         gate = {}
+        tiles = [(g, t) for g in range(HG) for t in range(PACK)]
+        ring = ["work4", "work5", "work3"]
 
-        def stage2(g, t):
-            times_site(g, t)
+        def times_site(i):
+            g, t = tiles[i]
+            gate[i] = late.tile([P, S], F32, name="gate", tag=ring[i % 3], align_bytes=64)
+            for j in range(JH):
+                toks = slice(NB * j, NB * (j + 1))
+                nc.gpsimd.tensor_tensor(out=gate[i][:, toks], in0=h_sb[g, j][:, t, :], in1=site_sb[g, t][:, toks], op=ALU.mult)
+
+        def stage2(i):
+            g, t = tiles[i]
             mixed = [psum.tile([P, NB], F32, name="acc", tag="acc") for j in range(JH)]
             c0 = PASS * g + P * t
             for a in range(HG):
@@ -247,36 +262,30 @@ def tile_list_tapping_panel_contrast_kernel(
                         start=(a == 0), stop=(a == HG - 1),
                     )
             for j in range(JH):
-                part = site_sb[g, t][:, NB * j : NB * (j + 1)]
+                part = gate[i][:, NB * j : NB * (j + 1)]
                 nc.vector.tensor_tensor(out=part, in0=mixed[j][:], in1=part, op=ALU.add)
-            gate[g, t] = late.tile([P, S], F32, name="gate", tag="gate", bufs=6)
-            nc.scalar.activation(out=gate[g, t][:], in_=site_sb[g, t][:], func=ACT.Sigmoid)
+            nc.scalar.activation(out=gate[i][:], in_=gate[i][:], func=ACT.Sigmoid)
 
-        y_sb = {}
+        y_sb = [late.tile([P, PACK, PAIRS], F32, name="y%d" % g, align_bytes=64) for g in range(HG)]
+        y_bf = [late.tile([P, PAIRS * PACK], BF16, name="ybf%d" % g, align_bytes=64) for g in range(HG)]
         yq = [late.tile([P, PAIRS], U32, name="yq%d" % g, align_bytes=64) for g in range(HG)]
         ys = [late.tile([P, PAIRS], U8, name="ys%d" % g, align_bytes=64) for g in range(HG)]
         y_rows = out_0.rearrange("(g p t) m -> g p t m", p=P, t=PACK)
 
-        def contrast(g, t, lo, hi):
+        def contrast(i, lo, hi):
+            g, t = tiles[i]
             n = hi - lo
-            if t == 0:
-                y_sb[g, lo] = late.tile([P, PACK, n], F32, name="y%d_%d" % (g, lo), align_bytes=64)
             rest = late.tile([P, n], F32, name="rest", tag="rest", bufs=2)
             diff = late.tile([P, n], F32, name="diff", tag="diff", bufs=3)
-            nc.vector.tensor_copy(rest[:], gate[g, t][:].indirect(pos2_sb[:, lo // 16 : hi // 16]))
-            nc.vector.tensor_tensor(diff[:], gate[g, t][:].indirect(pos1_sb[:, lo // 16 : hi // 16]), rest[:], ALU.subtract)
-            nc.scalar.activation(out=y_sb[g, lo][:, t, :], in_=diff[:], func=ACT.Copy, scale=span_sb[:, g, t : t + 1])
-            nc.sync.dma_start(out=y_rows[g][:, t, lo:hi], in_=y_sb[g, lo][:, t, :])
-
-        y_bf = {}
-
-        def weave_y(g, lo, hi, engine):
-            n = hi - lo
-            y_bf[g, lo] = late.tile([P, n * PACK], BF16, name="ybf%d_%d" % (g, lo), align_bytes=64)
-            weave(y_bf[g, lo][:], y_sb[g, lo][:], 0, n, engine)
+            nc.vector.tensor_copy(rest[:], gate[i][:].indirect(pos2_sb[:, lo // 16 : hi // 16]))
+            nc.vector.tensor_tensor(diff[:], gate[i][:].indirect(pos1_sb[:, lo // 16 : hi // 16]), rest[:], ALU.subtract)
+            nc.scalar.activation(out=y_sb[g][:, t, lo:hi], in_=diff[:], func=ACT.Copy, scale=span_sb[:, g, t : t + 1])
+            nc.sync.dma_start(out=y_rows[g][:, t, lo:hi], in_=y_sb[g][:, t, lo:hi])
 
         def planes(g, lo, hi):
-            nc.vector.quantize_mx(out=yq[g][:, lo:hi].bitcast(FP8X4), scales=ys[g][:, lo:hi], in_=y_bf[g, lo][:])
+            nc.vector.quantize_mx(
+                out=yq[g][:, lo:hi].bitcast(FP8X4), scales=ys[g][:, lo:hi], in_=y_bf[g][:, PACK * lo : PACK * hi]
+            )
             words = out_1[g].rearrange("p m t -> p (m t)").bitcast(I32)
             nc.sync.dma_start(out=words[:, lo:hi], in_=yq[g][:, lo:hi].bitcast(I32))
             if hi == PAIRS:
@@ -288,26 +297,22 @@ def tile_list_tapping_panel_contrast_kernel(
                     )
 
         half = PAIRS // 2
-        stage2(0, 0)
-        for t in range(PACK):
-            if t + 1 < PACK:
-                stage2(0, t + 1)
-            else:
-                stage2(1, 0)
-            contrast(0, t, 0, PAIRS)
-        weave_y(0, 0, PAIRS, "s")
-        for t in range(PACK):
-            if t + 1 < PACK:
-                stage2(1, t + 1)
-            else:
-                contrast(1, 0, half, PAIRS)
-            contrast(1, t, 0, half)
-            if t == 1:
+        last = len(tiles) - 1
+        for i in range(3):
+            times_site(i)
+        stage2(0)
+        for i in range(last):
+            stage2(i + 1)
+            contrast(i, 0, PAIRS)
+            if i + 3 <= last:
+                times_site(i + 3)
+            if i == PACK - 1:
+                weave(y_bf[0][:], y_sb[0][:], 0, PAIRS, "s")
+            if i == PACK + 1:
                 planes(0, 0, PAIRS)
-        weave_y(1, 0, half, "s")
-        contrast(1, 1, half, PAIRS)
-        contrast(1, 2, half, PAIRS)
+        contrast(last, 0, half)
+        weave(y_bf[1][:], y_sb[1][:], 0, half, "s")
+        contrast(last, half, PAIRS)
         planes(1, 0, half)
-        contrast(1, 3, half, PAIRS)
-        weave_y(1, half, PAIRS, "v")
+        weave(y_bf[1][:], y_sb[1][:], half, PAIRS, "v")
         planes(1, half, PAIRS)

@@ -53,7 +53,7 @@ def tile_list_tapping_panel_contrast_kernel(
             tabs = et("tabs", [P, T], U8)
             w2w_raw = et("w2w_raw", [P, HG, 2 * H], U8)
             w2s_raw = et("w2s_raw", [P, HG, H], U8)
-            w1_raw = {(b, a): et("w1raw%d%d" % (b, a), [P, PACK, PASS], F32) for b in range(HG) for a in range(KP)}
+            w1_raw = {(b, a): early.tile([P, PACK, PASS], F32, name="w1raw", tag="w1raw", bufs=5, align_bytes=64) for b in range(HG) for a in range(KP)}
 
             vw = [kt("vw%d" % a, [P, S], U32) for a in range(KP)]
             vs = kt("vs", [P, S], U8)
@@ -66,7 +66,7 @@ def tile_list_tapping_panel_contrast_kernel(
             hq = {(b, j): kt("hq%d%d" % (b, j), [P, NB], U32) for b in range(HG) for j in range(JH)}
             hs = {(b, j): kt("hs%d%d" % (b, j), [P, NB], U8) for b in range(HG) for j in range(JH)}
 
-            nc.vector.memset(tabs[:].bitcast(I32), 0)
+            nc.gpsimd.memset(tabs[:].bitcast(I32), 0)
             nc.vector.memset(w2s_raw[:].rearrange("p a c -> p (a c)").bitcast(I32), 0)
             nc.vector.memset(warm[:, 0:1], 0.0)
             nc.scalar.activation(out=warm[:, 1:2], in_=warm[:, 0:1], func=ACT.Sigmoid)
@@ -85,19 +85,19 @@ def tile_list_tapping_panel_contrast_kernel(
             nc.sync.dma_start(offs_sb[:], offs)
             nc.sync.dma_start(out=w2w_raw[:].bitcast(I32), in_=w2_words.rearrange("a p c -> p a c").bitcast(I32))
             for q in range(4):
-                nc.sync.dma_start(
+                nc.gpsimd.dma_start(
                     out=tabs[32 * q : 32 * q + 4 * KP, :].bitcast(I32),
                     in_=tab_scales[:, 4 * q : 4 * q + 4, :].bitcast(I32),
                 )
             load_w1(0, 0)
-            for q in range(4):
+            for r in range(4):
                 nc.sync.dma_start(
-                    out=w2s_raw[32 * q : 32 * q + 4, :, :].bitcast(I32),
-                    in_=w2_scales[:, 4 * q : 4 * q + 4, :].rearrange("a r c -> r a c").bitcast(I32),
+                    out=w2s_raw[r:P:32, :, :].bitcast(I32),
+                    in_=w2_scales[:, r:16:4, :].rearrange("a q c -> q a c").bitcast(I32),
                 )
-            load_tab(1)
             load_vec(floor_sb, floor_v)
             load_vec(gain_sb, gain)
+            load_tab(1)
             load_w1(0, 1)
             load_tab(2)
             load_w1(0, 2)
@@ -114,23 +114,21 @@ def tile_list_tapping_panel_contrast_kernel(
 
             w1_bf = {}
 
-            def cast_w1(b, a, vector_slots):
-                tile = early.tile([P, PASS * PACK], BF16, name="w1bf", tag="w1bf", bufs=2, align_bytes=64)
-                w1_bf[b, a] = tile
-                dst = tile[:].rearrange("p (t m j) -> p m j t", t=PACK, j=PACK)
+            def cast_w1(b, a, shared):
                 src = w1_raw[b, a][:].rearrange("p j (m t) -> p m j t", t=PACK)
-                if vector_slots > 0:
-                    nc.vector.tensor_copy(out=dst[:, :, :, 0:vector_slots], in_=src[:, :, :, 0:vector_slots])
-                if vector_slots < PACK:
-                    nc.scalar.copy(out=dst[:, :, :, vector_slots:PACK], in_=src[:, :, :, vector_slots:PACK])
+                if shared:
+                    parts = [(0, 2, "w1bf_lo", nc.vector.tensor_copy), (2, PACK, "w1bf_hi", nc.scalar.copy)]
+                else:
+                    parts = [(0, PACK, "w1bf", nc.scalar.copy)]
+                w1_bf[b, a] = []
+                for lo, hi, tag, copy in parts:
+                    tile = early.tile([P, (hi - lo) * PASS], BF16, name="w1bf", tag=tag, bufs=2, align_bytes=64)
+                    copy(out=tile[:].rearrange("p (t m j) -> p m j t", m=P, j=PACK), in_=src[:, :, :, lo:hi])
+                    w1_bf[b, a].append((P * lo, P * hi, tile))
 
-            def quant_w1(b, a, parts=1):
-                n = PASS // parts
-                for lo in range(0, PASS, n):
-                    nc.vector.quantize_mx(
-                        out=w1q[b, a][:, lo : lo + n].bitcast(FP8X4), scales=w1s[b, a][:, lo : lo + n],
-                        in_=w1_bf[b, a][:, PACK * lo : PACK * (lo + n)],
-                    )
+            def quant_w1(b, a):
+                for lo, hi, tile in w1_bf[b, a]:
+                    nc.vector.quantize_mx(out=w1q[b, a][:, lo:hi].bitcast(FP8X4), scales=w1s[b, a][:, lo:hi], in_=tile[:])
 
             def gather_words(a):
                 nc.vector.tensor_copy(vw[a][:], tabw[a][:].indirect(offs_sb[:]))
@@ -171,25 +169,28 @@ def tile_list_tapping_panel_contrast_kernel(
                 else:
                     nc.scalar.copy(out=d, in_=s)
 
-            def weave_h(b, j, vector_cols):
-                pool = late if (b, j) == (1, 1) else keep
-                tile = pool.tile([P, NB * PACK], BF16, name="hbf", tag="work%d" % (JH * b + j), align_bytes=64)
-                h_bf[b, j] = tile
-                for lo in range(0, vector_cols, 256):
-                    weave(tile[:], h_sb[b, j][:], lo, min(lo + 256, vector_cols), "v")
-                if vector_cols < NB:
-                    weave(tile[:], h_sb[b, j][:], vector_cols, NB, "s")
+            def weave_h(b, j, shared):
+                if shared:
+                    parts = [(0, NB // 2, late, "hbf_lo", "v"), (NB // 2, NB, late, "pick2", "s")]
+                else:
+                    parts = [(0, NB, keep, "hbf%d%d" % (b, j), "s")]
+                h_bf[b, j] = []
+                for lo, hi, pool, tag, engine in parts:
+                    tile = pool.tile([P, (hi - lo) * PACK], BF16, name="hbf", tag=tag, align_bytes=64)
+                    weave(tile[:], h_sb[b, j][:, :, lo:hi], 0, hi - lo, engine)
+                    h_bf[b, j].append((lo, hi, tile))
 
             def quant_h(b, j):
-                nc.vector.quantize_mx(out=hq[b, j][:].bitcast(FP8X4), scales=hs[b, j][:], in_=h_bf[b, j][:])
+                for lo, hi, tile in h_bf[b, j]:
+                    nc.vector.quantize_mx(out=hq[b, j][:, lo:hi].bitcast(FP8X4), scales=hs[b, j][:, lo:hi], in_=tile[:])
 
             gather_words(0)
-            cast_w1(0, 0, 0)
+            cast_w1(0, 0, False)
             nc.vector.tensor_copy(vs[:], tabs[:].indirect(offs_sb[:]))
             quant_w1(0, 0)
             nc.vector.tensor_copy(
-                out=w2w[:].rearrange("p a (g t m e) -> p (a g) m t e", g=HG, t=PACK, e=2),
-                in_=w2w_raw[:].rearrange("p a (g m t e) -> p (a g) m t e", g=HG, t=PACK, e=2),
+                out=w2w[:].bitcast(U16).rearrange("p a (g t m) -> p (a g) m t", g=HG, t=PACK),
+                in_=w2w_raw[:].bitcast(U16).rearrange("p a (g m t) -> p (a g) m t", g=HG, t=PACK),
             )
             nc.vector.tensor_copy(
                 out=w2s[:].rearrange("p a (g t m) -> p (a g) m t", g=HG, t=PACK),
@@ -197,26 +198,26 @@ def tile_list_tapping_panel_contrast_kernel(
             )
             stage1_all(0, 0)
             gather_words(1)
-            cast_w1(0, 1, 0)
+            cast_w1(0, 1, False)
             quant_w1(0, 1)
             stage1_all(0, 1)
             gather_words(2)
-            cast_w1(0, 2, 3)
-            quant_w1(0, 2, 2)
+            cast_w1(0, 2, True)
+            quant_w1(0, 2)
             stage1_all(0, 2)
 
-            cast_w1(1, 0, 0)
+            cast_w1(1, 0, False)
             for t in range(PACK):
                 features(0, 0, t)
             quant_w1(1, 0)
-            cast_w1(1, 1, 0)
+            cast_w1(1, 1, False)
             for t in range(PACK):
                 features(0, 1, t)
             for t in range(PACK):
                 stage1(1, 0, 0, t, False)
             quant_w1(1, 1)
-            cast_w1(1, 2, 3)
-            quant_w1(1, 2, 2)
+            cast_w1(1, 2, True)
+            quant_w1(1, 2)
             for a in range(1, KP):
                 for t in range(PACK):
                     stage1(1, a, 0, t, a == KP - 1)
@@ -225,29 +226,33 @@ def tile_list_tapping_panel_contrast_kernel(
                     stage1(1, a, 1, t, a == 1)
         late = ctx.enter_context(tc.tile_pool(name="late", bufs=1))
 
-        weave_h(0, 0, 0)
+        weave_h(0, 0, False)
         for t in range(PACK):
             features(1, 0, t)
-        weave_h(0, 1, 0)
+        weave_h(0, 1, False)
         for t in range(PACK):
             features(1, 1, t)
-        weave_h(1, 0, 0)
+        weave_h(1, 0, False)
         quant_h(0, 0)
         quant_h(0, 1)
-        weave_h(1, 1, 512)
+        weave_h(1, 1, True)
         quant_h(1, 0)
         quant_h(1, 1)
 
-        gate = {}
         tiles = [(g, t) for g in range(HG) for t in range(PACK)]
-        ring = ["work4", "work5", "work3"]
+        last = len(tiles) - 1
+        half = PAIRS // 2
+        depth = 4
+        cross, gate, rest = {}, {}, {}
 
         def times_site(i):
             g, t = tiles[i]
-            gate[i] = late.tile([P, S], F32, name="gate", tag=ring[i % 3], align_bytes=64)
             for j in range(JH):
-                toks = slice(NB * j, NB * (j + 1))
-                nc.gpsimd.tensor_tensor(out=gate[i][:, toks], in0=h_sb[g, j][:, t, :], in1=site_sb[g, t][:, toks], op=ALU.mult)
+                tag = ("pick%d" if j == 0 else "pair%d") % (i % depth)
+                cross[i, j] = late.tile([P, NB], F32, name="cross", tag=tag, align_bytes=64)
+                nc.gpsimd.tensor_tensor(
+                    out=cross[i, j][:], in0=h_sb[g, j][:, t, :], in1=site_sb[g, t][:, NB * j : NB * (j + 1)], op=ALU.mult
+                )
 
         def stage2(i):
             g, t = tiles[i]
@@ -261,30 +266,38 @@ def tile_list_tapping_panel_contrast_kernel(
                         rhs=hq[a, j][:].bitcast(FP8X4), rhs_scale=hs[a, j][:],
                         start=(a == 0), stop=(a == HG - 1),
                     )
+            gate[i] = late.tile([P, S], F32, name="gate", tag="gate", bufs=depth, align_bytes=64)
             for j in range(JH):
-                part = gate[i][:, NB * j : NB * (j + 1)]
-                nc.vector.tensor_tensor(out=part, in0=mixed[j][:], in1=part, op=ALU.add)
+                nc.vector.tensor_tensor(out=gate[i][:, NB * j : NB * (j + 1)], in0=mixed[j][:], in1=cross[i, j][:], op=ALU.add)
             nc.scalar.activation(out=gate[i][:], in_=gate[i][:], func=ACT.Sigmoid)
 
         y_sb = [late.tile([P, PACK, PAIRS], F32, name="y%d" % g, align_bytes=64) for g in range(HG)]
-        y_bf = [late.tile([P, PAIRS * PACK], BF16, name="ybf%d" % g, align_bytes=64) for g in range(HG)]
+        y_bf = {}
+
+        def weave_y(g, lo, hi, engine):
+            y_bf[g, lo] = late.tile([P, (hi - lo) * PACK], BF16, name="ybf%d_%d" % (g, lo), align_bytes=64)
+            weave(y_bf[g, lo][:], y_sb[g][:, :, lo:hi], 0, hi - lo, engine)
+
         yq = [late.tile([P, PAIRS], U32, name="yq%d" % g, align_bytes=64) for g in range(HG)]
         ys = [late.tile([P, PAIRS], U8, name="ys%d" % g, align_bytes=64) for g in range(HG)]
         y_rows = out_0.rearrange("(g p t) m -> g p t m", p=P, t=PACK)
 
+        def pick_rest(i, lo, hi):
+            tag = "pick%d" % (i % depth) if lo == 0 else "pick_tail"
+            rest[i, lo] = late.tile([P, hi - lo], F32, name="rest", tag=tag, align_bytes=64)
+            nc.vector.tensor_copy(rest[i, lo][:], gate[i][:].indirect(pos2_sb[:, lo // 16 : hi // 16]))
+
         def contrast(i, lo, hi):
             g, t = tiles[i]
-            n = hi - lo
-            rest = late.tile([P, n], F32, name="rest", tag="rest", bufs=2)
-            diff = late.tile([P, n], F32, name="diff", tag="diff", bufs=3)
-            nc.vector.tensor_copy(rest[:], gate[i][:].indirect(pos2_sb[:, lo // 16 : hi // 16]))
-            nc.vector.tensor_tensor(diff[:], gate[i][:].indirect(pos1_sb[:, lo // 16 : hi // 16]), rest[:], ALU.subtract)
+            tag = "pair%d" % ((i + 2) % depth) if lo == 0 else "pair_tail"
+            diff = late.tile([P, hi - lo], F32, name="diff", tag=tag, align_bytes=64)
+            nc.vector.tensor_tensor(diff[:], gate[i][:].indirect(pos1_sb[:, lo // 16 : hi // 16]), rest[i, lo][:], ALU.subtract)
             nc.scalar.activation(out=y_sb[g][:, t, lo:hi], in_=diff[:], func=ACT.Copy, scale=span_sb[:, g, t : t + 1])
             nc.sync.dma_start(out=y_rows[g][:, t, lo:hi], in_=y_sb[g][:, t, lo:hi])
 
         def planes(g, lo, hi):
             nc.vector.quantize_mx(
-                out=yq[g][:, lo:hi].bitcast(FP8X4), scales=ys[g][:, lo:hi], in_=y_bf[g][:, PACK * lo : PACK * hi]
+                out=yq[g][:, lo:hi].bitcast(FP8X4), scales=ys[g][:, lo:hi], in_=y_bf[g, lo][:]
             )
             words = out_1[g].rearrange("p m t -> p (m t)").bitcast(I32)
             nc.sync.dma_start(out=words[:, lo:hi], in_=yq[g][:, lo:hi].bitcast(I32))
@@ -296,23 +309,27 @@ def tile_list_tapping_panel_contrast_kernel(
                         in_=ys[g][32 * q : 32 * q + 4, :].bitcast(I32),
                     )
 
-        half = PAIRS // 2
-        last = len(tiles) - 1
-        for i in range(3):
+        for i in range(depth):
             times_site(i)
         stage2(0)
-        for i in range(last):
-            stage2(i + 1)
+        stage2(1)
+        pick_rest(0, 0, PAIRS)
+        for i in range(last - 1):
+            stage2(i + 2)
             contrast(i, 0, PAIRS)
-            if i + 3 <= last:
-                times_site(i + 3)
+            if i + depth <= last:
+                times_site(i + depth)
+            pick_rest(i + 1, 0, PAIRS)
             if i == PACK - 1:
-                weave(y_bf[0][:], y_sb[0][:], 0, PAIRS, "s")
+                weave_y(0, 0, PAIRS, "s")
             if i == PACK + 1:
                 planes(0, 0, PAIRS)
+        pick_rest(last, 0, half)
+        contrast(last - 1, 0, PAIRS)
+        pick_rest(last, half, PAIRS)
         contrast(last, 0, half)
-        weave(y_bf[1][:], y_sb[1][:], 0, half, "s")
+        weave_y(1, 0, half, "s")
         contrast(last, half, PAIRS)
         planes(1, 0, half)
-        weave(y_bf[1][:], y_sb[1][:], half, PAIRS, "v")
+        weave_y(1, half, PAIRS, "v")
         planes(1, half, PAIRS)

@@ -36,7 +36,7 @@ def tile_list_tapping_panel_contrast_kernel(
         with tc.tile_pool(name="early", bufs=1) as early:
 
             def kt(name, shape, dtype):
-                return keep.tile(shape, dtype, name=name, align_bytes=64)
+                return keep.tile(shape, dtype, name=name, tag=name, align_bytes=64)
 
             def et(name, shape, dtype):
                 return early.tile(shape, dtype, name=name, align_bytes=64)
@@ -62,9 +62,11 @@ def tile_list_tapping_panel_contrast_kernel(
             w1q = {(b, a): kt("w1q%d%d" % (b, a), [P, PASS], U32) for b in range(HG) for a in range(KP)}
             w1s = {(b, a): kt("w1s%d%d" % (b, a), [P, PASS], U8) for b in range(HG) for a in range(KP)}
             site_sb = {(b, t): kt("site%d%d" % (b, t), [P, S], F32) for b in range(HG) for t in range(PACK)}
-            h_sb = {(b, j): kt("h%d%d" % (b, j), [P, PACK, NB], F32) for b in range(HG) for j in range(JH)}
+            h_sb = [kt("h%d" % b, [P, JH, PACK, NB], F32) for b in range(HG)]
             hq = {(b, j): kt("hq%d%d" % (b, j), [P, NB], U32) for b in range(HG) for j in range(JH)}
-            hs = {(b, j): kt("hs%d%d" % (b, j), [P, NB], U8) for b in range(HG) for j in range(JH)}
+            hs = {(1, j): kt("hs1%d" % j, [P, NB], U8) for j in range(JH)}
+            hs[0, 0] = keep.tile([P, NB], U8, name="hs00", tag="floor_sb", align_bytes=64)
+            hs[0, 1] = keep.tile([P, NB], U8, name="hs01", tag="gain_sb", align_bytes=64)
 
             nc.gpsimd.memset(tabs[:].bitcast(I32), 0)
             nc.vector.memset(w2s_raw[:].rearrange("p a c -> p (a c)").bitcast(I32), 0)
@@ -154,7 +156,7 @@ def tile_list_tapping_panel_contrast_kernel(
 
             def features(b, j, t):
                 nc.vector.tensor_scalar(
-                    out=h_sb[b, j][:, t, :], in0=flow[b, j, t][:],
+                    out=h_sb[b][:, j, t, :], in0=flow[b, j, t][:],
                     scalar1=floor_sb[:, b, t : t + 1], scalar2=gain_sb[:, b, t : t + 1],
                     op0=ALU.max, op1=ALU.mult,
                 )
@@ -171,13 +173,13 @@ def tile_list_tapping_panel_contrast_kernel(
 
             def weave_h(b, j, shared):
                 if shared:
-                    parts = [(0, NB // 2, late, "hbf_lo", "v"), (NB // 2, NB, late, "pick2", "s")]
+                    parts = [(0, NB // 2, late, "hbf_lo", "v"), (NB // 2, NB, late, "turn6", "s")]
                 else:
                     parts = [(0, NB, keep, "hbf%d%d" % (b, j), "s")]
                 h_bf[b, j] = []
                 for lo, hi, pool, tag, engine in parts:
                     tile = pool.tile([P, (hi - lo) * PACK], BF16, name="hbf", tag=tag, align_bytes=64)
-                    weave(tile[:], h_sb[b, j][:, :, lo:hi], 0, hi - lo, engine)
+                    weave(tile[:], h_sb[b][:, j, :, lo:hi], 0, hi - lo, engine)
                     h_bf[b, j].append((lo, hi, tile))
 
             def quant_h(b, j):
@@ -247,12 +249,10 @@ def tile_list_tapping_panel_contrast_kernel(
 
         def times_site(i):
             g, t = tiles[i]
-            for j in range(JH):
-                tag = ("pick%d" if j == 0 else "pair%d") % (i % depth)
-                cross[i, j] = late.tile([P, NB], F32, name="cross", tag=tag, align_bytes=64)
-                nc.gpsimd.tensor_tensor(
-                    out=cross[i, j][:], in0=h_sb[g, j][:, t, :], in1=site_sb[g, t][:, NB * j : NB * (j + 1)], op=ALU.mult
-                )
+            cross[i] = late.tile([P, JH, NB], F32, name="cross", tag="turn%d" % ((i + depth) % len(tiles)), align_bytes=64)
+            nc.gpsimd.tensor_tensor(
+                out=cross[i][:], in0=h_sb[g][:, :, t, :], in1=site_sb[g, t][:].rearrange("p (j c) -> p j c", j=JH), op=ALU.mult
+            )
 
         def stage2(i):
             g, t = tiles[i]
@@ -266,9 +266,9 @@ def tile_list_tapping_panel_contrast_kernel(
                         rhs=hq[a, j][:].bitcast(FP8X4), rhs_scale=hs[a, j][:],
                         start=(a == 0), stop=(a == HG - 1),
                     )
-            gate[i] = late.tile([P, S], F32, name="gate", tag="gate", bufs=depth, align_bytes=64)
+            gate[i] = late.tile([P, S], F32, name="gate", tag="turn%d" % i, align_bytes=64)
             for j in range(JH):
-                nc.vector.tensor_tensor(out=gate[i][:, NB * j : NB * (j + 1)], in0=mixed[j][:], in1=cross[i, j][:], op=ALU.add)
+                nc.vector.tensor_tensor(out=gate[i][:, NB * j : NB * (j + 1)], in0=mixed[j][:], in1=cross[i][:, j, :], op=ALU.add)
             nc.scalar.activation(out=gate[i][:], in_=gate[i][:], func=ACT.Sigmoid)
 
         y_sb = [late.tile([P, PACK, PAIRS], F32, name="y%d" % g, align_bytes=64) for g in range(HG)]
@@ -283,13 +283,12 @@ def tile_list_tapping_panel_contrast_kernel(
         y_rows = out_0.rearrange("(g p t) m -> g p t m", p=P, t=PACK)
 
         def pick_rest(i, lo, hi):
-            tag = "pick%d" % (i % depth) if lo == 0 else "pick_tail"
-            rest[i, lo] = late.tile([P, hi - lo], F32, name="rest", tag=tag, align_bytes=64)
+            rest[i, lo] = late.tile([P, hi - lo], F32, name="rest", tag="rest", bufs=3, align_bytes=64)
             nc.vector.tensor_copy(rest[i, lo][:], gate[i][:].indirect(pos2_sb[:, lo // 16 : hi // 16]))
 
         def contrast(i, lo, hi):
             g, t = tiles[i]
-            tag = "pair%d" % ((i + 2) % depth) if lo == 0 else "pair_tail"
+            tag = "turn%d" % ((i + 2 + depth) % len(tiles)) if lo == 0 else "pair_tail"
             diff = late.tile([P, hi - lo], F32, name="diff", tag=tag, align_bytes=64)
             nc.vector.tensor_tensor(diff[:], gate[i][:].indirect(pos1_sb[:, lo // 16 : hi // 16]), rest[i, lo][:], ALU.subtract)
             nc.scalar.activation(out=y_sb[g][:, t, lo:hi], in_=diff[:], func=ACT.Copy, scale=span_sb[:, g, t : t + 1])
@@ -328,8 +327,8 @@ def tile_list_tapping_panel_contrast_kernel(
         contrast(last - 1, 0, PAIRS)
         pick_rest(last, half, PAIRS)
         contrast(last, 0, half)
-        weave_y(1, 0, half, "s")
         contrast(last, half, PAIRS)
-        planes(1, 0, half)
+        weave_y(1, 0, half, "v")
         weave_y(1, half, PAIRS, "v")
+        planes(1, 0, half)
         planes(1, half, PAIRS)

from contextlib import ExitStack

import concourse.mybir as mybir

K, T, S, PAIRS, H = 1536, 4096, 1024, 512, 1024
FLOPS = 2 * K * H * S + 2 * H * H * S

F32 = mybir.dt.float32
BF16 = mybir.dt.bfloat16
I32 = mybir.dt.int32
U32 = mybir.dt.uint32
U16 = mybir.dt.uint16
U8 = mybir.dt.uint8
FP8X4 = mybir.dt.float8_e4m3fn_x4
FP4X4 = mybir.dt.float4_e2m1fn_x4
ALU = mybir.AluOpType
ACT = mybir.ActivationFunctionType

P = 128
PACK = 4
PASS = P * PACK
NB = 512
KP = K // PASS
HG = H // PASS
JH = S // NB


def tile_list_tapping_panel_contrast_kernel(
    tc, tab_words, tab_scales, offs, pos1, pos2, w1, floor_v, gain, w2_words, w2_scales, site, span,
    out_0, out_1, out_2,
):
    nc = tc.nc
    with ExitStack() as ctx:
        keep = ctx.enter_context(tc.tile_pool(name="keep", bufs=1))
        psum = ctx.enter_context(tc.psum_pool(name="psum", bufs=8))
        with tc.tile_pool(name="early", bufs=1) as early:

            def kt(name, shape, dtype):
                return keep.tile(shape, dtype, name=name, tag=name, align_bytes=64)

            def et(name, shape, dtype):
                return early.tile(shape, dtype, name=name, align_bytes=64)

            offs_sb = keep.tile([P, S // 16], U16, name="offs_sb")
            pos1_sb = keep.tile([P, PAIRS // 16], U16, name="pos1_sb")
            pos2_sb = keep.tile([P, PAIRS // 16], U16, name="pos2_sb")
            floor_sb = kt("floor_sb", [P, HG, PACK], F32)
            gain_sb = kt("gain_sb", [P, HG, PACK], F32)
            span_sb = kt("span_sb", [P, HG, PACK], F32)
            warm = kt("warm", [P, 2], F32)

            tabw = [et("tabw%d" % a, [P, T], U32) for a in range(KP)]
            tabs = et("tabs", [P, T], U8)
            w2w_raw = et("w2w_raw", [P, HG, 2 * H], U8)
            w2s_raw = et("w2s_raw", [P, HG, H], U8)
            w1_raw = {(b, a): early.tile([P, PACK, PASS], F32, name="w1raw", tag="w1raw", bufs=5, align_bytes=64) for b in range(HG) for a in range(KP)}

            vw = [kt("vw%d" % a, [P, S], U32) for a in range(KP)]
            vs = kt("vs", [P, S], U8)
            w2w = kt("w2w", [P, HG, 2 * H], U8)
            w2s = kt("w2s", [P, HG, H], U8)
            w1q = {(b, a): kt("w1q%d%d" % (b, a), [P, PASS], U32) for b in range(HG) for a in range(KP)}
            w1s = {(b, a): kt("w1s%d%d" % (b, a), [P, PASS], U8) for b in range(HG) for a in range(KP)}
            site_sb = {(b, t): kt("site%d%d" % (b, t), [P, S], F32) for b in range(HG) for t in range(PACK)}
            h_sb = [kt("h%d" % b, [P, JH, PACK, NB], F32) for b in range(HG)]
            hq = {(b, j): kt("hq%d%d" % (b, j), [P, NB], U32) for b in range(HG) for j in range(JH)}
            hs = {(1, j): kt("hs1%d" % j, [P, NB], U8) for j in range(JH)}
            hs[0, 0] = keep.tile([P, NB], U8, name="hs00", tag="floor_sb", align_bytes=64)
            hs[0, 1] = keep.tile([P, NB], U8, name="hs01", tag="gain_sb", align_bytes=64)

            nc.gpsimd.memset(tabs[:].bitcast(I32), 0)
            nc.vector.memset(w2s_raw[:].rearrange("p a c -> p (a c)").bitcast(I32), 0)
            nc.vector.memset(warm[:, 0:1], 0.0)
            nc.scalar.activation(out=warm[:, 1:2], in_=warm[:, 0:1], func=ACT.Sigmoid)

            def load_tab(a):
                nc.sync.dma_start(out=tabw[a][:].bitcast(I32), in_=tab_words[a].rearrange("p t i -> p (t i)").bitcast(I32))

            def load_w1(b, a):
                rows = w1[PASS * a : PASS * (a + 1), PASS * b : PASS * (b + 1)]
                nc.sync.dma_start(out=w1_raw[b, a][:], in_=rows.rearrange("(p j) c -> p j c", j=PACK))

            def load_vec(dst, vec):
                nc.sync.dma_start(out=dst[:], in_=vec.rearrange("(b p t) -> p b t", p=P, t=PACK))

            load_tab(0)
            nc.sync.dma_start(offs_sb[:], offs)
            nc.sync.dma_start(out=w2w_raw[:].bitcast(I32), in_=w2_words.rearrange("a p c -> p a c").bitcast(I32))
            for q in range(4):
                nc.gpsimd.dma_start(
                    out=tabs[32 * q : 32 * q + 4 * KP, :].bitcast(I32),
                    in_=tab_scales[:, 4 * q : 4 * q + 4, :].bitcast(I32),
                )
            load_w1(0, 0)
            for r in range(4):
                nc.sync.dma_start(
                    out=w2s_raw[r:P:32, :, :].bitcast(I32),
                    in_=w2_scales[:, r:16:4, :].rearrange("a q c -> q a c").bitcast(I32),
                )
            load_vec(floor_sb, floor_v)
            load_vec(gain_sb, gain)
            load_tab(1)
            load_w1(0, 1)
            load_tab(2)
            load_w1(0, 2)
            for a in range(KP):
                load_w1(1, a)
            site_rows = site.rearrange("(b p t) j -> b t p j", p=P, t=PACK)
            for b in range(HG):
                for t in range(PACK):
                    nc.sync.dma_start(out=site_sb[b, t][:], in_=site_rows[b, t])
                if b == 0:
                    nc.sync.dma_start(pos1_sb[:], pos1)
                    nc.sync.dma_start(pos2_sb[:], pos2)
                    load_vec(span_sb, span)

            w1_bf = {}

            def cast_w1(b, a, shared):
                src = w1_raw[b, a][:].rearrange("p j (m t) -> p m j t", t=PACK)
                if shared:
                    parts = [(0, 2, "w1bf_lo", nc.vector.tensor_copy), (2, PACK, "w1bf_hi", nc.scalar.copy)]
                else:
                    parts = [(0, PACK, "w1bf", nc.scalar.copy)]
                w1_bf[b, a] = []
                for lo, hi, tag, copy in parts:
                    tile = early.tile([P, (hi - lo) * PASS], BF16, name="w1bf", tag=tag, bufs=2, align_bytes=64)
                    copy(out=tile[:].rearrange("p (t m j) -> p m j t", m=P, j=PACK), in_=src[:, :, :, lo:hi])
                    w1_bf[b, a].append((P * lo, P * hi, tile))

            def quant_w1(b, a):
                for lo, hi, tile in w1_bf[b, a]:
                    nc.vector.quantize_mx(out=w1q[b, a][:, lo:hi].bitcast(FP8X4), scales=w1s[b, a][:, lo:hi], in_=tile[:])

            def gather_words(a):
                nc.vector.tensor_copy(vw[a][:], tabw[a][:].indirect(offs_sb[:]))

            flow = {}

            def stage1(b, a, j, t, stop):
                if a == 0:
                    flow[b, j, t] = psum.tile([P, NB], F32, name="acc", tag="acc")
                cols = slice(P * t, P * (t + 1))
                toks = slice(NB * j, NB * (j + 1))
                nc.tensor.matmul_mx(
                    out=flow[b, j, t][:],
                    lhsT=w1q[b, a][:, cols].bitcast(FP8X4), lhsT_scale=w1s[b, a][:, cols],
                    rhs=vw[a][:, toks].bitcast(FP8X4), rhs_scale=vs[4 * a : P, toks],
                    start=(a == 0), stop=stop,
                )

            def stage1_all(b, a):
                for j in range(JH):
                    for t in range(PACK):
                        stage1(b, a, j, t, a == KP - 1)

            def features(b, j, t):
                nc.vector.tensor_scalar(
                    out=h_sb[b][:, j, t, :], in0=flow[b, j, t][:],
                    scalar1=floor_sb[:, b, t : t + 1], scalar2=gain_sb[:, b, t : t + 1],
                    op0=ALU.max, op1=ALU.mult,
                )

            h_bf = {}

            def weave(dst, src, lo, hi, engine):
                d = dst.rearrange("p (c i t) -> p c t i", i=4, t=PACK)[:, lo // 4 : hi // 4]
                s = src.rearrange("p t (c i) -> p c t i", i=4)[:, lo // 4 : hi // 4]
                if engine == "v":
                    nc.vector.tensor_copy(out=d, in_=s)
                else:
                    nc.scalar.copy(out=d, in_=s)

            def weave_h(b, j, shared):
                if shared:
                    parts = [(0, NB // 2, late, "hbf_lo", "v"), (NB // 2, NB, late, "turn6", "s")]
                else:
                    parts = [(0, NB, keep, "hbf%d%d" % (b, j), "s")]
                h_bf[b, j] = []
                for lo, hi, pool, tag, engine in parts:
                    tile = pool.tile([P, (hi - lo) * PACK], BF16, name="hbf", tag=tag, align_bytes=64)
                    weave(tile[:], h_sb[b][:, j, :, lo:hi], 0, hi - lo, engine)
                    h_bf[b, j].append((lo, hi, tile))

            def quant_h(b, j):
                for lo, hi, tile in h_bf[b, j]:
                    nc.vector.quantize_mx(out=hq[b, j][:, lo:hi].bitcast(FP8X4), scales=hs[b, j][:, lo:hi], in_=tile[:])

            gather_words(0)
            cast_w1(0, 0, False)
            nc.vector.tensor_copy(vs[:], tabs[:].indirect(offs_sb[:]))
            quant_w1(0, 0)
            nc.vector.tensor_copy(
                out=w2w[:].bitcast(U16).rearrange("p a (g t m) -> p (a g) m t", g=HG, t=PACK),
                in_=w2w_raw[:].bitcast(U16).rearrange("p a (g m t) -> p (a g) m t", g=HG, t=PACK),
            )
            nc.vector.tensor_copy(
                out=w2s[:].rearrange("p a (g t m) -> p (a g) m t", g=HG, t=PACK),
                in_=w2s_raw[:].rearrange("p a (g m t) -> p (a g) m t", g=HG, t=PACK),
            )
            stage1_all(0, 0)
            gather_words(1)
            cast_w1(0, 1, False)
            quant_w1(0, 1)
            stage1_all(0, 1)
            gather_words(2)
            cast_w1(0, 2, True)
            quant_w1(0, 2)
            stage1_all(0, 2)

            cast_w1(1, 0, False)
            for t in range(PACK):
                features(0, 0, t)
            quant_w1(1, 0)
            cast_w1(1, 1, False)
            for t in range(PACK):
                features(0, 1, t)
            for t in range(PACK):
                stage1(1, 0, 0, t, False)
            quant_w1(1, 1)
            cast_w1(1, 2, True)
            quant_w1(1, 2)
            for a in range(1, KP):
                for t in range(PACK):
                    stage1(1, a, 0, t, a == KP - 1)
            for t in range(PACK):
                for a in (0, 2, 1):
                    stage1(1, a, 1, t, a == 1)
        late = ctx.enter_context(tc.tile_pool(name="late", bufs=1))

        weave_h(0, 0, False)
        for t in range(PACK):
            features(1, 0, t)
        weave_h(0, 1, False)
        for t in range(PACK):
            features(1, 1, t)
        weave_h(1, 0, False)
        quant_h(0, 0)
        quant_h(0, 1)
        weave_h(1, 1, True)
        quant_h(1, 0)
        quant_h(1, 1)

        tiles = [(g, t) for g in range(HG) for t in range(PACK)]
        last = len(tiles) - 1
        half = PAIRS // 2
        depth = 4
        cross, gate, rest = {}, {}, {}

        def times_site(i):
            g, t = tiles[i]
            cross[i] = late.tile([P, JH, NB], F32, name="cross", tag="turn%d" % ((i + depth) % len(tiles)), align_bytes=64)
            nc.gpsimd.tensor_tensor(
                out=cross[i][:], in0=h_sb[g][:, :, t, :], in1=site_sb[g, t][:].rearrange("p (j c) -> p j c", j=JH), op=ALU.mult
            )

        def stage2(i):
            g, t = tiles[i]
            mixed = [psum.tile([P, NB], F32, name="acc", tag="acc") for j in range(JH)]
            c0 = PASS * g + P * t
            for a in range(HG):
                for j in range(JH):
                    nc.tensor.matmul_mx(
                        out=mixed[j][:],
                        lhsT=w2w[:, a, 2 * c0 : 2 * (c0 + P)].bitcast(FP4X4), lhsT_scale=w2s[:, a, c0 : c0 + P],
                        rhs=hq[a, j][:].bitcast(FP8X4), rhs_scale=hs[a, j][:],
                        start=(a == 0), stop=(a == HG - 1),
                    )
            gate[i] = late.tile([P, S], F32, name="gate", tag="turn%d" % i, align_bytes=64)
            for j in range(JH):
                nc.vector.tensor_tensor(out=gate[i][:, NB * j : NB * (j + 1)], in0=mixed[j][:], in1=cross[i][:, j, :], op=ALU.add)
            nc.scalar.activation(out=gate[i][:], in_=gate[i][:], func=ACT.Sigmoid)

        y_sb = [late.tile([P, PACK, PAIRS], F32, name="y%d" % g, align_bytes=64) for g in range(HG)]
        y_bf = {}

        def weave_y(g, lo, hi, engine):
            y_bf[g, lo] = late.tile([P, (hi - lo) * PACK], BF16, name="ybf%d_%d" % (g, lo), align_bytes=64)
            weave(y_bf[g, lo][:], y_sb[g][:, :, lo:hi], 0, hi - lo, engine)

        yq = [late.tile([P, PAIRS], U32, name="yq%d" % g, align_bytes=64) for g in range(HG)]
        ys = [late.tile([P, PAIRS], U8, name="ys%d" % g, align_bytes=64) for g in range(HG)]
        y_rows = out_0.rearrange("(g p t) m -> g p t m", p=P, t=PACK)

        def pick_rest(i, lo, hi):
            rest[i, lo] = late.tile([P, hi - lo], F32, name="rest", tag="rest", bufs=3, align_bytes=64)
            nc.vector.tensor_copy(rest[i, lo][:], gate[i][:].indirect(pos2_sb[:, lo // 16 : hi // 16]))

        def contrast(i, lo, hi):
            g, t = tiles[i]
            tag = "turn%d" % ((i + 2 + depth) % len(tiles)) if lo == 0 else "pair_tail"
            diff = late.tile([P, hi - lo], F32, name="diff", tag=tag, align_bytes=64)
            nc.vector.tensor_tensor(diff[:], gate[i][:].indirect(pos1_sb[:, lo // 16 : hi // 16]), rest[i, lo][:], ALU.subtract)
            nc.scalar.activation(out=y_sb[g][:, t, lo:hi], in_=diff[:], func=ACT.Copy, scale=span_sb[:, g, t : t + 1])
            nc.sync.dma_start(out=y_rows[g][:, t, lo:hi], in_=y_sb[g][:, t, lo:hi])

        def planes(g, lo, hi):
            nc.vector.quantize_mx(
                out=yq[g][:, lo:hi].bitcast(FP8X4), scales=ys[g][:, lo:hi], in_=y_bf[g, lo][:]
            )
            words = out_1[g].rearrange("p m t -> p (m t)").bitcast(I32)
            nc.sync.dma_start(out=words[:, lo:hi], in_=yq[g][:, lo:hi].bitcast(I32))
            if hi == PAIRS:
                for q in range(4):
                    queue = nc.sync if q % 2 == 0 else nc.scalar
                    queue.dma_start(
                        out=out_2[g, 4 * q : 4 * q + 4, :].bitcast(I32),
                        in_=ys[g][32 * q : 32 * q + 4, :].bitcast(I32),
                    )

        for i in range(depth):
            times_site(i)
        stage2(0)
        stage2(1)
        pick_rest(0, 0, PAIRS)
        for i in range(last - 1):
            stage2(i + 2)
            contrast(i, 0, PAIRS)
            if i + depth <= last:
                times_site(i + depth)
            pick_rest(i + 1, 0, PAIRS)
            if i == PACK - 1:
                weave_y(0, 0, PAIRS, "s")
            if i == PACK + 1:
                planes(0, 0, PAIRS)
        pick_rest(last, 0, half)
        contrast(last - 1, 0, PAIRS)
        pick_rest(last, half, PAIRS)
        contrast(last, 0, half)
        contrast(last, half, PAIRS)
        weave_y(1, 0, half, "v")
        weave_y(1, half, PAIRS, "v")
        planes(1, 0, half)
        planes(1, half, PAIRS)
